import numpy as np, ml_dtypes
CORES = [97,101,225,229,353,357,481,485]
N = 8
R, TK = 16, 512
def setup_inputs(rng):
    u = (rng.standard_normal((N, 128, R), dtype=np.float32) / 11).astype(ml_dtypes.bfloat16)
    return {"x": rng.standard_normal((N, 128, TK), dtype=np.float32).astype(ml_dtypes.bfloat16), "u": u, "ut": u.transpose(0, 2, 1).copy(), "vt": rng.standard_normal((N, R, 128), dtype=np.float32).astype(ml_dtypes.bfloat16)}
def setup_inputs_big(rng):
    d = setup_inputs(rng)
    for k in ("x", "u", "ut", "vt"): d[k] = (d[k].astype(np.float32) * 1024.0).astype(d[k].dtype)
    return d
def setup_inputs_small(rng):
    d = setup_inputs(rng)
    for k in ("x", "u", "ut", "vt"): d[k] = (d[k].astype(np.float32) * (1 / 1024.0)).astype(d[k].dtype)
    return d
def setup_inputs_apart(rng):
    d = setup_inputs(rng)
    f = (10.0 ** rng.permutation(np.linspace(-1.5, 1.5, N))).astype(np.float32).reshape(N, 1, 1)
    for k in ("x", "u", "ut", "vt"): d[k] = (d[k].astype(np.float32) * f).astype(d[k].dtype)
    return d
def tie_inputs(x):
    x = dict(x)
    x["ut"] = x["u"].transpose(0, 2, 1).copy()
    return x
def reference(x, u, ut, vt):
    X, U, VT = x.astype(np.float64), u.astype(np.float64), vt.astype(np.float64)
    y = np.stack([sum(VT[j].T @ (U[j].T @ X[r]) for j in range(N)) for r in range(N)])
    return {"y": y.astype(ml_dtypes.bfloat16 if x.dtype != np.float64 else np.float64)}

from concourse.bass import DstId, RemoteDMATransfer

SCRATCH = {
    "G": ("dram", [8, 128, 32], "bfloat16"),
    "UT": ("sbuf", [128, 128], "bfloat16"),
    "VT": ("sbuf", [128, 128], "bfloat16"),
    "X": ("sbuf", [128, 512], "bfloat16"),
    "W": ("sbuf", [128, 128], "bfloat16"),
    "Y": ("sbuf", [128, 512], "bfloat16"),
    "Wp": ("psum", [128, 512], "float32"),
    "Ya": ("psum", [128, 512], "float32"),
    "Yb": ("psum", [128, 512], "float32"),
}
SEMAPHORES = ["ld", "xs", "rel", "near", "far", "sent", "nl", "fl", "mw", "cw", "ma", "mb", "cy", "done"]


def _plan(cores, topo):
    near = {s: [d for d in cores if d != s and topo.may_write(s, d)] for s in cores}
    far = {s: [d for d in cores if d != s and not topo.may_write(s, d)] for s in cores}
    pos = {d: {s: i for i, s in enumerate([d] + near[d] + far[d])} for d in cores}
    relay = {}
    for s in cores:
        cand = [m for m in near[s] if topo.die(m) == topo.die(s) and all(topo.may_write(m, f) for f in far[s])]
        relay[s] = min(cand, key=lambda m: (cores.index(m) - cores.index(s)) % len(cores))
    return near, far, pos, relay


def _bits(engines):
    return sum(1 << e for e in engines)


def rank_program(g, core, T, topo):
    if T.rank_of(core) is None:
        return
    cores = list(T.cores)
    near, far, pos, relay = _plan(cores, topo)
    sem = T.sem
    n_near = 1 + len(near[core])
    n_all = len(cores)
    R = T.ut.shape[0]
    half = T.G.shape[1] // 2
    k_near, k_all = R * n_near, R * n_all

    common = topo.mask(core, near[core][0])
    for d in near[core]:
        common &= topo.mask(core, d)
    eng = [e for e in range(common.bit_length()) if common >> e & 1][::2]
    m_a, m_b, n_eng = _bits(eng[0:2]), _bits(eng[2:4]), 2

    def dst_id(d):
        rid, pid = topo.addr(d, core)
        return DstId(rid=rid, pnc=pid)

    g.sync.dma_start(T.G[0, 0:half, :], T.ut[:]).then_inc(sem.ld, 16)
    g.scalar.dma_start(T.G[0, half:2 * half, :], T.vt[:]).then_inc(sem.ld, 16)
    g.sync.dma_start(T.X[:], T.x[:]).then_inc(sem.xs, 16)
    for q, buf, lo in ((g.sync, T.UT, 0), (g.scalar, T.VT, half)):
        q.wait_ge(sem.ld, 32)
        q.wait_ge(sem.rel, n_eng)
        q.wait_ge(sem.near, n_eng * (len(near[core]) - 1))
        q.dma_start(buf[0:k_near, :], T.G[0:n_near, lo:lo + half, :]).then_inc(sem.nl, 16)
        q.wait_ge(sem.far, n_eng * len(far[core]))
        q.dma_start(buf[k_near:k_all, :], T.G[n_near:n_all, lo:lo + half, :]).then_inc(sem.fl, 16)

    g.wait_ge(sem.ld, 32)
    first = relay[core]
    rid, pid = topo.addr(first, core)
    g.remote_dma(out_ap=T.G[pos[first][core]], in_ap=T.G[0], remote_sem=sem.rel, local_sem=sem.sent,
                 pid=pid, routing_id=rid, dma_engine_mask=m_a)
    rest = [d for d in near[core] if d != first]
    groups = ((m_b, rest[0::2]), (m_a, rest[1::2]))
    g.remote_dma_fused([RemoteDMATransfer(dst_ids=[dst_id(d) for d in ds], dma_engine_mask=m, remote_sem=sem.near,
                                          srcs=[T.G[0]], dsts=[T.G[pos[d][core]] for d in ds], alu_op=0)
                        for m, ds in groups], local_sem=sem.sent)
    src = [s for s in cores if relay[s] == core][0]
    g.wait_ge(sem.rel, n_eng)
    g.remote_dma_fused([RemoteDMATransfer(dst_ids=[dst_id(f)], dma_engine_mask=m, remote_sem=sem.far,
                                          srcs=[T.G[pos[core][src]]], dsts=[T.G[pos[f][src]]], alu_op=0)
                        for m, f in zip((m_a, m_b), far[src])], local_sem=sem.sent)
    g.wait_ge(sem.sent, n_eng * (1 + len(groups) + len(far[src])))

    cols = T.x.shape[1] // 2
    wp = T.Wp[:, 0:T.W.shape[1]]
    g.tensor.wait_ge(sem.nl, 32)
    g.tensor.matmul(wp, T.UT[0:k_near, :], T.VT[0:k_near, :], start=True, stop=False)
    g.tensor.wait_ge(sem.fl, 32)
    g.tensor.matmul(wp, T.UT[k_near:k_all, :], T.VT[k_near:k_all, :], start=False, stop=True).then_inc(sem.mw, 1)
    g.vector.wait_ge(sem.mw, 1)
    g.vector.tensor_copy(T.W[:], wp).then_inc(sem.cw, 1)
    g.tensor.wait_ge(sem.xs, 16)
    g.tensor.wait_ge(sem.cw, 1)
    for i, (ps, s) in enumerate(((T.Ya, sem.ma), (T.Yb, sem.mb))):
        g.tensor.matmul(ps[:, 0:cols], T.W[:], T.X[:, i * cols:(i + 1) * cols], start=True, stop=True).then_inc(s, 1)
        g.vector.wait_ge(s, 1)
        g.vector.tensor_copy(T.Y[:, i * cols:(i + 1) * cols], ps[:, 0:cols]).then_inc(sem.cy, 1)
    g.sync.wait_ge(sem.cy, 2)
    g.sync.dma_start(T.y[:], T.Y[:]).then_inc(sem.done, 16)
    g.sync.wait_ge(sem.done, 16)
